import numpy as np
import ml_dtypes


def mxq(x, axis, fmt="e4m3"):
    dtype, down = {"e4m3": (ml_dtypes.float8_e4m3fn, 7), "e5m2": (ml_dtypes.float8_e5m2, 14)}[fmt]
    v = np.moveaxis(np.asarray(x, np.float32).astype(ml_dtypes.bfloat16).astype(np.float64), axis, -1)
    blocks = v.reshape(v.shape[:-1] + (-1, 32))
    amax = np.abs(blocks).max(-1, keepdims=True)
    byte = np.maximum(np.where(amax > 0, np.frexp(amax)[1] - 1 + 127, 0) - down, 1)
    scale = np.exp2(byte - 127.0)
    codes = (blocks / scale).astype(np.float32).astype(dtype).astype(np.float64)
    return np.moveaxis((codes * scale).reshape(v.shape), -1, axis)


WIDE = False


def mx_kscale(k):
    if not WIDE:
        return np.ones(k)
    levels = np.array([10, -10, 5, -5, 0])
    if k % 512:
        return np.exp2(np.random.permutation(np.resize(levels, k // 32))).repeat(32)
    a = np.empty((k // 512, 16))
    for p in range(k // 512):
        a[p, :8] = np.random.permutation(np.resize(levels, 8))
        for g in range(8):
            far = levels[np.abs(levels - a[p, g]) >= 10]
            a[p, g + 8] = far[np.random.randint(len(far))]
    return np.exp2(a.ravel()).repeat(32)


def f64(x):
    return np.asarray(x).astype(np.float64)


def striped(idx):
    return np.tile(idx.reshape(-1, 16).T, (8, 1)).astype(np.uint16)


def unstriped(offs):
    return offs[:16].T.reshape(-1).astype(np.int64)


def striped8(idx):
    return np.concatenate([x.reshape(-1, 16).T for x in idx]).astype(np.uint16)


def runs(offs, k):
    lists = np.stack([offs[16 * r : 16 * r + 16].T.reshape(-1) for r in range(8)]).astype(np.int64)
    return lists[np.arange(k) % 512 // 64]


def pack_weight(w):
    k, n = w.shape
    w = f64(np.asarray(w, np.float32).astype(ml_dtypes.bfloat16)).reshape(k // 32, 32, n)
    amax = np.abs(w).max(1)
    byte = np.clip(np.where(amax > 0, np.frexp(amax)[1] - 1 + 127 - 7, 1), 1, 254)
    scaled = (w * np.exp2(127.0 - byte)[:, None, :]).reshape(k, n).astype(np.float32)
    words = np.ascontiguousarray(scaled.reshape(k // 512, 128, 4, n).transpose(0, 1, 3, 2)).astype(ml_dtypes.float8_e4m3fn).view(np.uint8)
    return words, np.ascontiguousarray(byte.astype(np.uint8).reshape(k // 512, 16, n))


def unpack_weight(words, scales):
    g, p, n, _ = words.shape
    vals = np.ascontiguousarray(words).view(ml_dtypes.float8_e4m3fn).astype(np.float64) * np.repeat(np.exp2(scales.astype(np.float64) - 127.0), 8, axis=1)[..., None]
    return vals.transpose(0, 1, 3, 2).reshape(g * 512, n)


K, T, S, N, H = 512, 2048, 512, 512, 512


def setup_inputs():
    n = np.random.standard_normal
    s = mx_kscale(K)[:, None]
    u = mx_kscale(H)
    packed_xT = pack_weight(n((K, T)) * s)
    return {
        "x_words": packed_xT[0],
        "x_scales": packed_xT[1],
        "w1": (n((K, H)) / np.sqrt(K) / s).astype(np.float32),
        "gn": (np.random.uniform(0.5, 1.5, (H, 1)) * u[:, None]).astype(np.float32),
        "w2": (n((H, N)) / np.sqrt(H) / u[:, None]).astype(np.float32),
        "offs": striped(np.random.permutation(T)[:S]),
        "p1": striped8(np.stack([np.random.permutation(S) for _ in range(8)])),
        "p2": striped8(np.stack([np.random.permutation(S) for _ in range(8)])),
    }


def reference(x_words, x_scales, w1, gn, w2, offs, p1, p2):
    xq = unpack_weight(x_words, x_scales)[:, unstriped(offs)]
    y = mxq(f64(w1), 0, "e4m3").T @ xq
    d1 = y[np.arange(H)[:, None], runs(p1, H)] - y
    d2 = y[np.arange(H)[:, None], runs(p2, H)] - y
    z = f64(gn) * (y + 0.25 * ((np.exp(-0.5 * ((d1) ** 2))) * d1) + 0.25 * ((np.exp(-0.5 * ((d2) ** 2))) * d2))
    return mxq(f64(w2), 0, "e4m3").T @ mxq(z, 0, "e4m3")

@@ -1,0 +1,220 @@
+from contextlib import ExitStack
+
+import concourse.mybir as mybir
+from concourse.masks import make_identity
+
+K, T, S, N, H = 512, 2048, 512, 512, 512
+FLOPS = 2 * K * H * S + 2 * H * N * S
+
+F32 = mybir.dt.float32
+BF16 = mybir.dt.bfloat16
+I32 = mybir.dt.int32
+U32 = mybir.dt.uint32
+U16 = mybir.dt.uint16
+U8 = mybir.dt.uint8
+FP8X4 = mybir.dt.float8_e4m3fn_x4
+ALU = mybir.AluOpType
+ACT = mybir.ActivationFunctionType
+
+P = 128
+PACK = 4
+CHUNKS = ((0, 128), (128, 256), (384, 128))
+
+
+def tile_picked_perona_none_p_kernel(tc, x_words, x_scales, w1, gn, w2, offs, p1, p2, out):
+    nc = tc.nc
+    with ExitStack() as ctx:
+        keep = ctx.enter_context(tc.tile_pool(name="keep", bufs=1))
+        psum = ctx.enter_context(tc.psum_pool(name="psum", bufs=1))
+
+        offs_t = keep.tile([P, S // 16], U16, name="offs_t")
+        p1_t = keep.tile([P, S // 16], U16, name="p1_t")
+        p2_t = keep.tile([P, S // 16], U16, name="p2_t")
+        w1_raw = keep.tile([P, PACK, H], F32, name="w1_raw")
+        w2_raw = keep.tile([P, PACK, N], F32, name="w2_raw")
+        xw = keep.tile([P, T], I32, name="xw")
+        xs = keep.tile([P, T], U8, name="xs")
+        gain = keep.tile([P, PACK], F32, name="gain")
+
+        nc.vector.memset(xs[:].bitcast(I32), 0)
+        warm_in = keep.tile([P, 1], F32, name="warm_in")
+        warm_out = keep.tile([P, 1], F32, name="warm_out")
+        nc.vector.memset(warm_in[:], 0.0)
+        nc.scalar.activation(warm_out[:], warm_in[:], ACT.Exp)
+
+        nc.sync.dma_start(offs_t[:], offs)
+        nc.sync.dma_start(w1_raw[:], w1.rearrange("(p j) h -> p j h", j=PACK))
+        nc.sync.dma_start(xw[:], x_words[0].rearrange("p n t -> p (n t)").bitcast(I32))
+        for q in range(4):
+            nc.scalar.dma_start(xs[32 * q : 32 * q + 4, :].bitcast(I32), x_scales[0, 4 * q : 4 * q + 4, :].bitcast(I32))
+        nc.scalar.dma_start(gain[:], gn.rearrange("(p t) o -> p (t o)", t=PACK))
+        nc.sync.dma_start(p1_t[:], p1)
+        nc.sync.dma_start(p2_t[:], p2)
+        nc.sync.dma_start(w2_raw[:], w2.rearrange("(p j) n -> p j n", j=PACK))
+
+        ident = keep.tile([P, P], F32, name="ident")
+        make_identity(nc, ident[:])
+
+        xg_scales = keep.tile([P, S], U8, name="xg_scales", align_bytes=64)
+        nc.vector.tensor_copy(xg_scales[:], xs[:].indirect(offs_t[:]))
+
+        gain_safe = keep.tile([P, PACK], F32, name="gain_safe")
+        inv_gain = keep.tile([P, PACK], F32, name="inv_gain")
+        nc.vector.scalar_tensor_tensor(gain_safe[:], gain[:], 0.0, gain[:], ALU.is_equal, ALU.add)
+        nc.vector.reciprocal(inv_gain[:], gain_safe[:])
+
+        w1_codes, w1_scales = [], []
+        w1_view = w1_raw[:].rearrange("p j (m t) -> p m t j", t=PACK)
+        for h in range(2):
+            grouped = keep.tile([P, 2, P, PACK], BF16, name=f"w1_grouped{h}", align_bytes=64)
+            dst = grouped[:].rearrange("p t m j -> p m t j")
+            src = w1_view[:, :, 2 * h : 2 * h + 2, :]
+            if h == 0:
+                nc.vector.tensor_copy(dst, src)
+            else:
+                nc.scalar.copy(dst, src)
+            codes = keep.tile([P, 2 * P], U32, name=f"w1_codes{h}", align_bytes=64)
+            scales = keep.tile([P, 2 * P], U8, name=f"w1_scales{h}", align_bytes=64)
+            nc.vector.quantize_mx(out=codes[:].bitcast(FP8X4), scales=scales[:], in_=grouped[:].rearrange("p t m j -> p (t m j)"))
+            w1_codes.append(codes)
+            w1_scales.append(scales)
+
+        xg_words = keep.tile([P, S], U32, name="xg_words", align_bytes=64)
+        half = S // 2
+        for a in range(2):
+            nc.vector.tensor_copy(
+                xg_words[:, a * half : (a + 1) * half],
+                xw[:].bitcast(U32).indirect(offs_t[:, a * half // 16 : (a + 1) * half // 16]),
+            )
+
+        yg = [keep.tile([P, S], F32, name=f"yg{t}") for t in range(PACK)]
+        first = CHUNKS[0][1]
+        y_head = [keep.tile([P, first], F32, name=f"y_head{t}") for t in range(PACK)]
+        y_rest = [keep.tile([P, S - first], F32, name=f"y_rest{t}") for t in range(PACK)]
+
+        def first_product(t, c0, c1):
+            bank = psum.tile([P, 512], F32, name="bank", tag="mx", bufs=4)
+            cols = slice((t % 2) * P, (t % 2 + 1) * P)
+            nc.tensor.matmul_mx(
+                out=bank[:, 0 : c1 - c0],
+                lhsT=w1_codes[t // 2][:, cols].bitcast(FP8X4),
+                lhsT_scale=w1_scales[t // 2][:, cols],
+                rhs=xg_words[:, c0:c1].bitcast(FP8X4),
+                rhs_scale=xg_scales[:, c0:c1],
+                start=True,
+                stop=True,
+            )
+            nc.scalar.activation(yg[t][:, c0:c1], bank[:, 0 : c1 - c0], ACT.Copy, scale=gain[:, t : t + 1])
+
+        first_product(0, 0, half)
+        nc.vector.tensor_copy(y_head[0][:], yg[0][:, 0:first])
+        first_product(0, half, S)
+        nc.sync.dma_start(y_rest[0][:], yg[0][:, first:S])
+        for t in range(1, PACK):
+            first_product(t, 0, S)
+            nc.sync.dma_start(y_rest[t][:], yg[t][:, first:S])
+
+        w2_grouped = keep.tile([P, N, PACK], BF16, name="w2_grouped", align_bytes=64)
+        w2_codes = keep.tile([P, N], U32, name="w2_codes", align_bytes=64)
+        w2_scales = keep.tile([P, N], U8, name="w2_scales", align_bytes=64)
+
+        def cast_w2(a):
+            cols = slice(a * 256, (a + 1) * 256)
+            nc.vector.tensor_copy(
+                w2_grouped[:, cols, :].rearrange("p (c i) t -> p c t i", i=4),
+                w2_raw[:, :, cols].rearrange("p t (c i) -> p c t i", i=4),
+            )
+
+        def quantize_w2():
+            nc.vector.quantize_mx(out=w2_codes[:].bitcast(FP8X4), scales=w2_scales[:], in_=w2_grouped[:].rearrange("p n t -> p (n t)"))
+
+        diffs, weights, sums = {}, {}, {}
+
+        def gather(c, t):
+            j0, n = CHUNKS[c]
+            plain = y_head[t][:] if c == 0 else y_rest[t][:, j0 - first : j0 - first + n]
+            d = keep.tile([P, 2 * n], F32, name=f"d{c}_{t}")
+            for s, lists in enumerate((p1_t, p2_t)):
+                nc.vector.tensor_tensor(
+                    d[:, s * n : (s + 1) * n], yg[t][:].indirect(lists[:, j0 // 16 : (j0 + n) // 16]), plain, ALU.subtract
+                )
+            diffs[c, t] = d
+
+        def weigh(c, t):
+            n = CHUNKS[c][1]
+            sq = keep.tile([P, 2 * n], F32, name=f"sq{c}_{t}")
+            e = keep.tile([P, 2 * n], F32, name=f"e{c}_{t}")
+            nc.scalar.activation(sq[:], diffs[c, t][:], ACT.Square, scale=inv_gain[:, t : t + 1])
+            nc.scalar.activation(e[:], sq[:], ACT.Exp, scale=-0.5)
+            weights[c, t] = e
+
+        def pull(c, t):
+            j0, n = CHUNKS[c]
+            m = keep.tile([P, 2 * n], F32, name=f"m{c}_{t}")
+            nc.vector.scalar_tensor_tensor(m[:], weights[c, t][:], 0.25, diffs[c, t][:], ALU.mult, ALU.mult)
+            for b in range(n // P):
+                if t == 0:
+                    sums[c, b] = psum.tile([P, PACK, P], F32, name="zt", tag="zt", bufs=3)
+                terms = (
+                    yg[t][:, j0 + b * P : j0 + (b + 1) * P],
+                    m[:, b * P : (b + 1) * P],
+                    m[:, n + b * P : n + (b + 1) * P],
+                )
+                for i, term in enumerate(terms):
+                    nc.tensor.matmul(sums[c, b][:, t, :], term, ident[:], start=(i == 0), stop=(i == 2), is_transpose=True)
+
+        def finish(c):
+            j0, n = CHUNKS[c]
+            blocks = n // P
+            back = psum.tile([P, 2, 2, P], F32, name="back", tag="back", bufs=1)
+            for b in range(blocks):
+                zt = keep.tile([P, 2, P, 2], BF16, name=f"zt{c}_{b}")
+                nc.scalar.copy(zt[:], sums[c, b][:].rearrange("j (u e) p -> j u p e", e=2))
+                words = zt[:].rearrange("j u p e -> j (u p e)").bitcast(F32)
+                for u in range(2):
+                    nc.tensor.transpose(back[:, b, u, :], words[:, u * P : (u + 1) * P], ident[:])
+            z = keep.tile([P, n * PACK], BF16, name=f"z{c}", align_bytes=64)
+            nc.vector.tensor_copy(
+                z[:].bitcast(F32).rearrange("p (b j u) -> p b j u", b=blocks, u=2),
+                back[:, 0:blocks, :, :].rearrange("p b u j -> p b j u"),
+            )
+            z_codes = keep.tile([P, n], U32, name=f"z_codes{c}", align_bytes=64)
+            z_scales = keep.tile([P, n], U8, name=f"z_scales{c}", align_bytes=64)
+            nc.vector.quantize_mx(out=z_codes[:].bitcast(FP8X4), scales=z_scales[:], in_=z[:])
+            per_bank = 512 // n
+            for g in range(PACK // per_bank):
+                bank = psum.tile([P, 512], F32, name="bank", tag="mx", bufs=4)
+                for i in range(per_bank):
+                    rows = slice((g * per_bank + i) * P, (g * per_bank + i + 1) * P)
+                    nc.tensor.matmul_mx(
+                        out=bank[:, i * n : (i + 1) * n],
+                        lhsT=w2_codes[:, rows].bitcast(FP8X4),
+                        lhsT_scale=w2_scales[:, rows],
+                        rhs=z_codes[:].bitcast(FP8X4),
+                        rhs_scale=z_scales[:],
+                        start=True,
+                        stop=True,
+                    )
+                res = keep.tile([P, per_bank, n], F32, name=f"res{c}_{g}")
+                nc.scalar.copy(res[:].rearrange("p a j -> p (a j)"), bank[:])
+                r0 = g * per_bank * P
+                nc.sync.dma_start(out[r0 : r0 + per_bank * P, j0 : j0 + n].rearrange("(a p) j -> p a j", p=P), res[:])
+
+        units = [(c, t) for c in range(len(CHUNKS)) for t in range(PACK)]
+        for i in range(len(units) + 3):
+            if i + 1 < PACK:
+                nc.vector.tensor_copy(y_head[i + 1][:], yg[i + 1][:, 0:first])
+            if i < len(units):
+                gather(*units[i])
+            if i == 3:
+                cast_w2(0)
+            if i == 4:
+                cast_w2(1)
+            if i == 5:
+                quantize_w2()
+            if 1 <= i <= len(units):
+                weigh(*units[i - 1])
+            if 2 <= i <= len(units) + 1:
+                pull(*units[i - 2])
+            if i >= 3 and units[i - 3][1] == PACK - 1:
+                finish(units[i - 3][0])

@@ -18,7 +18,8 @@ ACT = mybir.ActivationFunctionType
 
 P = 128
 PACK = 4
-CHUNKS = ((0, 128), (128, 256), (384, 128))
+CHUNKS = ((0, 256), (256, 128), (384, 128))
+LEAD = 4
 
 
 def tile_picked_perona_none_p_kernel(tc, x_words, x_scales, w1, gn, w2, offs, p1, p2, out):
@@ -44,9 +45,9 @@ def tile_picked_perona_none_p_kernel(tc, x_words, x_scales, w1, gn, w2, offs, p1
 
         nc.sync.dma_start(offs_t[:], offs)
         nc.sync.dma_start(w1_raw[:], w1.rearrange("(p j) h -> p j h", j=PACK))
-        nc.sync.dma_start(xw[:], x_words[0].rearrange("p n t -> p (n t)").bitcast(I32))
         for q in range(4):
-            nc.scalar.dma_start(xs[32 * q : 32 * q + 4, :].bitcast(I32), x_scales[0, 4 * q : 4 * q + 4, :].bitcast(I32))
+            nc.sync.dma_start(xs[32 * q : 32 * q + 4, :].bitcast(I32), x_scales[0, 4 * q : 4 * q + 4, :].bitcast(I32))
+        nc.sync.dma_start(xw[:], x_words[0].rearrange("p n t -> p (n t)").bitcast(I32))
         nc.scalar.dma_start(gain[:], gn.rearrange("(p t) o -> p (t o)", t=PACK))
         nc.sync.dma_start(p1_t[:], p1)
         nc.sync.dma_start(p2_t[:], p2)
@@ -90,7 +91,7 @@ def tile_picked_perona_none_p_kernel(tc, x_words, x_scales, w1, gn, w2, offs, p1
         yg = [keep.tile([P, S], F32, name=f"yg{t}") for t in range(PACK)]
         first = CHUNKS[0][1]
         y_head = [keep.tile([P, first], F32, name=f"y_head{t}") for t in range(PACK)]
-        y_rest = [keep.tile([P, S - first], F32, name=f"y_rest{t}") for t in range(PACK)]
+        y_rest = keep.tile([P, PACK, S - first], F32, name="y_rest")
 
         def first_product(t, c0, c1):
             bank = psum.tile([P, 512], F32, name="bank", tag="mx", bufs=4)
@@ -109,62 +110,95 @@ def tile_picked_perona_none_p_kernel(tc, x_words, x_scales, w1, gn, w2, offs, p1
         first_product(0, 0, half)
         nc.vector.tensor_copy(y_head[0][:], yg[0][:, 0:first])
         first_product(0, half, S)
-        nc.sync.dma_start(y_rest[0][:], yg[0][:, first:S])
+        nc.sync.dma_start(y_rest[:, 0, :], yg[0][:, first:S])
         for t in range(1, PACK):
             first_product(t, 0, S)
-            nc.sync.dma_start(y_rest[t][:], yg[t][:, first:S])
+            nc.sync.dma_start(y_rest[:, t, :], yg[t][:, first:S])
 
-        w2_grouped = keep.tile([P, N, PACK], BF16, name="w2_grouped", align_bytes=64)
         w2_codes = keep.tile([P, N], U32, name="w2_codes", align_bytes=64)
         w2_scales = keep.tile([P, N], U8, name="w2_scales", align_bytes=64)
 
-        def cast_w2(a):
+        def quantize_w2(a):
             cols = slice(a * 256, (a + 1) * 256)
-            nc.vector.tensor_copy(
-                w2_grouped[:, cols, :].rearrange("p (c i) t -> p c t i", i=4),
-                w2_raw[:, :, cols].rearrange("p t (c i) -> p c t i", i=4),
-            )
+            grouped = keep.tile([P, 256 * PACK], BF16, name=f"w2_grouped{a}", align_bytes=64)
+            dst = grouped[:].rearrange("p (c i t) -> p c t i", i=4, t=PACK)
+            src = w2_raw[:, :, cols].rearrange("p t (c i) -> p c t i", i=4)
+            if a < 2:
+                nc.scalar.copy(dst, src)
+            else:
+                nc.vector.tensor_copy(dst, src)
+            nc.vector.quantize_mx(out=w2_codes[:, cols].bitcast(FP8X4), scales=w2_scales[:, cols], in_=grouped[:])
 
-        def quantize_w2():
-            nc.vector.quantize_mx(out=w2_codes[:].bitcast(FP8X4), scales=w2_scales[:], in_=w2_grouped[:].rearrange("p n t -> p (n t)"))
+        last = len(CHUNKS) - 1
+        units = [(c, (t,)) for c in range(3) for t in range(4)]
+        slots = [keep.tile([P, 512], F32, name=f"slot{i}") for i in range(len(units) + LEAD)]
+        sums, packed = {}, {}
 
-        diffs, weights, sums = {}, {}, {}
-
-        def gather(c, t):
+        def plain_y(c, t):
             j0, n = CHUNKS[c]
-            plain = y_head[t][:] if c == 0 else y_rest[t][:, j0 - first : j0 - first + n]
-            d = keep.tile([P, 2 * n], F32, name=f"d{c}_{t}")
-            for s, lists in enumerate((p1_t, p2_t)):
-                nc.vector.tensor_tensor(
-                    d[:, s * n : (s + 1) * n], yg[t][:].indirect(lists[:, j0 // 16 : (j0 + n) // 16]), plain, ALU.subtract
-                )
-            diffs[c, t] = d
+            return y_head[t][:] if c == 0 else y_rest[:, t, j0 - first : j0 - first + n]
 
-        def weigh(c, t):
+        def gather(i):
+            c, planes = units[i]
+            j0, n = CHUNKS[c]
+            for k, t in enumerate(planes):
+                for s, lists in enumerate((p1_t, p2_t)):
+                    nc.vector.tensor_tensor(
+                        slots[i][:, (2 * k + s) * n : (2 * k + s + 1) * n],
+                        yg[t][:].indirect(lists[:, j0 // 16 : (j0 + n) // 16]),
+                        plain_y(c, t),
+                        ALU.subtract,
+                    )
+
+        def weigh(i, cols):
+            c, planes = units[i]
+            step = (cols.stop - cols.start) // len(planes)
+            for k, t in enumerate(planes):
+                part = slice(cols.start + k * step, cols.start + (k + 1) * step)
+                nc.scalar.activation(slots[i + LEAD][:, part], slots[i][:, part], ACT.Square, scale=inv_gain[:, t : t + 1])
+            nc.scalar.activation(weights[i][:, cols], slots[i + LEAD][:, cols], ACT.Exp, scale=-0.5)
+
+        def pull(i, cols):
+            nc.vector.scalar_tensor_tensor(pulls[i][:, cols], weights[i][:, cols], 0.25, slots[i][:, cols], ALU.mult, ALU.mult)
+
+        def add_turned(i):
+            c, planes = units[i]
+            j0, n = CHUNKS[c]
+            for k, t in enumerate(planes):
+                for b in range(n // P):
+                    if t == 0:
+                        sums[c, b] = psum.tile([P, PACK, P], F32, name="zt", tag="zt", bufs=3)
+                    terms = (
+                        yg[t][:, j0 + b * P : j0 + (b + 1) * P],
+                        pulls[i][:, 2 * k * n + b * P : 2 * k * n + (b + 1) * P],
+                        pulls[i][:, (2 * k + 1) * n + b * P : (2 * k + 1) * n + (b + 1) * P],
+                    )
+                    for a, term in enumerate(terms):
+                        nc.tensor.matmul(sums[c, b][:, t, :], term, ident[:], start=(a == 0), stop=(a == 2), is_transpose=True)
+
+        n_last = CHUNKS[last][1]
+        m_last = keep.tile([P, PACK * 2 * n_last], F32, name="m_last")
+        m_view = m_last[:].rearrange("p (t s j) -> p t s j", t=PACK, s=2)
+        a_last = keep.tile([P, PACK, n_last], F32, name="a_last")
+        widths = [2 * len(planes) * CHUNKS[c][1] for c, planes in units]
+        weights = [keep.tile([P, w], F32, name=f"e{i}") for i, w in enumerate(widths)]
+        pulls = [
+            m_last[:, 2 * n_last * planes[0] : 2 * n_last * (planes[-1] + 1)] if c == last else keep.tile([P, widths[i]], F32, name=f"m{i}")
+            for i, (c, planes) in enumerate(units)
+        ]
+
+        def add_first(ts):
+            nc.vector.tensor_tensor(a_last[:, ts, :], m_view[:, ts, 0, :], y_rest[:, ts, S - first - n_last : S - first], ALU.add)
+
+        def quantize_z(c, z):
             n = CHUNKS[c][1]
-            sq = keep.tile([P, 2 * n], F32, name=f"sq{c}_{t}")
-            e = keep.tile([P, 2 * n], F32, name=f"e{c}_{t}")
-            nc.scalar.activation(sq[:], diffs[c, t][:], ACT.Square, scale=inv_gain[:, t : t + 1])
-            nc.scalar.activation(e[:], sq[:], ACT.Exp, scale=-0.5)
-            weights[c, t] = e
+            z_codes = keep.tile([P, n], U32, name=f"z_codes{c}", align_bytes=64)
+            z_scales = keep.tile([P, n], U8, name=f"z_scales{c}", align_bytes=64)
+            nc.vector.quantize_mx(out=z_codes[:].bitcast(FP8X4), scales=z_scales[:], in_=z[:])
+            packed[c] = (z_codes, z_scales)
 
-        def pull(c, t):
-            j0, n = CHUNKS[c]
-            m = keep.tile([P, 2 * n], F32, name=f"m{c}_{t}")
-            nc.vector.scalar_tensor_tensor(m[:], weights[c, t][:], 0.25, diffs[c, t][:], ALU.mult, ALU.mult)
-            for b in range(n // P):
-                if t == 0:
-                    sums[c, b] = psum.tile([P, PACK, P], F32, name="zt", tag="zt", bufs=3)
-                terms = (
-                    yg[t][:, j0 + b * P : j0 + (b + 1) * P],
-                    m[:, b * P : (b + 1) * P],
-                    m[:, n + b * P : n + (b + 1) * P],
-                )
-                for i, term in enumerate(terms):
-                    nc.tensor.matmul(sums[c, b][:, t, :], term, ident[:], start=(i == 0), stop=(i == 2), is_transpose=True)
-
-        def finish(c):
-            j0, n = CHUNKS[c]
+        def turn_back(c):
+            n = CHUNKS[c][1]
             blocks = n // P
             back = psum.tile([P, 2, 2, P], F32, name="back", tag="back", bufs=1)
             for b in range(blocks):
@@ -174,14 +208,18 @@ def tile_picked_perona_none_p_kernel(tc, x_words, x_scales, w1, gn, w2, offs, p1
                 for u in range(2):
                     nc.tensor.transpose(back[:, b, u, :], words[:, u * P : (u + 1) * P], ident[:])
             z = keep.tile([P, n * PACK], BF16, name=f"z{c}", align_bytes=64)
-            nc.vector.tensor_copy(
-                z[:].bitcast(F32).rearrange("p (b j u) -> p b j u", b=blocks, u=2),
-                back[:, 0:blocks, :, :].rearrange("p b u j -> p b j u"),
-            )
-            z_codes = keep.tile([P, n], U32, name=f"z_codes{c}", align_bytes=64)
-            z_scales = keep.tile([P, n], U8, name=f"z_scales{c}", align_bytes=64)
-            nc.vector.quantize_mx(out=z_codes[:].bitcast(FP8X4), scales=z_scales[:], in_=z[:])
-            per_bank = 512 // n
+            z_dst = z[:].bitcast(F32).rearrange("p (b j u) -> p b j u", b=blocks, u=2)
+            z_src = back[:, 0:blocks, :, :].rearrange("p b u j -> p b j u")
+            if c in ():
+                nc.vector.tensor_copy(z_dst, z_src)
+            else:
+                nc.scalar.copy(z_dst, z_src)
+            quantize_z(c, z)
+
+        def second_product(c, on_vector):
+            j0, n = CHUNKS[c]
+            z_codes, z_scales = packed[c]
+            per_bank = 2 if c == last else 512 // n
             for g in range(PACK // per_bank):
                 bank = psum.tile([P, 512], F32, name="bank", tag="mx", bufs=4)
                 for i in range(per_bank):
@@ -196,25 +234,51 @@ def tile_picked_perona_none_p_kernel(tc, x_words, x_scales, w1, gn, w2, offs, p1
                         stop=True,
                     )
                 res = keep.tile([P, per_bank, n], F32, name=f"res{c}_{g}")
-                nc.scalar.copy(res[:].rearrange("p a j -> p (a j)"), bank[:])
+                res_dst = res[:].rearrange("p a j -> p (a j)")
                 r0 = g * per_bank * P
-                nc.sync.dma_start(out[r0 : r0 + per_bank * P, j0 : j0 + n].rearrange("(a p) j -> p a j", p=P), res[:])
+                rows_out = out[r0 : r0 + per_bank * P, j0 : j0 + n].rearrange("(a p) j -> p a j", p=P)
+                if g in on_vector:
+                    nc.vector.tensor_copy(res_dst, bank[:, 0 : per_bank * n])
+                else:
+                    nc.scalar.copy(res_dst, bank[:, 0 : per_bank * n])
+                if c == last and g not in on_vector:
+                    nc.scalar.dma_start(rows_out, res[:])
+                else:
+                    nc.sync.dma_start(rows_out, res[:])
 
-        units = [(c, t) for c in range(len(CHUNKS)) for t in range(PACK)]
-        for i in range(len(units) + 3):
+        final = len(units) - 1
+        for i in range(len(units) + 1):
             if i + 1 < PACK:
                 nc.vector.tensor_copy(y_head[i + 1][:], yg[i + 1][:, 0:first])
-            if i < len(units):
-                gather(*units[i])
-            if i == 3:
-                cast_w2(0)
-            if i == 4:
-                cast_w2(1)
-            if i == 5:
-                quantize_w2()
-            if 1 <= i <= len(units):
-                weigh(*units[i - 1])
-            if 2 <= i <= len(units) + 1:
-                pull(*units[i - 2])
-            if i >= 3 and units[i - 3][1] == PACK - 1:
-                finish(units[i - 3][0])
+            if i <= final:
+                gather(i)
+            if 1 <= i <= final:
+                weigh(i - 1, slice(0, widths[i - 1]))
+            if i == 1:
+                quantize_w2(0)
+            if i == 2:
+                quantize_w2(1)
+            if i >= 2:
+                pull(i - 2, slice(0, widths[i - 2]))
+                if units[i - 2][0] < last:
+                    add_turned(i - 2)
+            if i >= 3 and units[i - 3][1][-1] == PACK - 1 and units[i - 3][0] < last:
+                turn_back(units[i - 3][0])
+            if i >= 4 and units[i - 4][1][-1] == PACK - 1 and units[i - 4][0] < last - 1:
+                second_product(units[i - 4][0], (0, 1))
+        weigh(final, slice(0, n_last))
+        weigh(final, slice(n_last, 2 * n_last))
+        pull(final, slice(0, n_last))
+        pull(final, slice(n_last, 2 * n_last))
+        add_first(slice(0, PACK - 1))
+        add_first(slice(PACK - 1, PACK))
+        z = keep.tile([P, n_last * PACK], BF16, name="z_last", align_bytes=64)
+        nc.vector.tensor_tensor(
+            z[:].rearrange("p (c i t) -> p c t i", i=4, t=PACK),
+            m_view[:, :, 1, :].rearrange("p t (c i) -> p c t i", i=4),
+            a_last[:].rearrange("p t (c i) -> p c t i", i=4),
+            ALU.add,
+        )
+        quantize_z(last, z)
+        second_product(last - 1, ())
+        second_product(last, (0,))

@@ -18,6 +18,9 @@ ACT = mybir.ActivationFunctionType
 
 P = 128
 PACK = 4
+BANK = 512
+GROUP = 16
+LINE = 4
 CHUNKS = ((0, 256), (256, 128), (384, 128))
 LEAD = 4
 
@@ -28,26 +31,37 @@ def tile_picked_perona_none_p_kernel(tc, x_words, x_scales, w1, gn, w2, offs, p1
         keep = ctx.enter_context(tc.tile_pool(name="keep", bufs=1))
         psum = ctx.enter_context(tc.psum_pool(name="psum", bufs=1))
 
-        offs_t = keep.tile([P, S // 16], U16, name="offs_t")
-        p1_t = keep.tile([P, S // 16], U16, name="p1_t")
-        p2_t = keep.tile([P, S // 16], U16, name="p2_t")
+        def product_bank():
+            return psum.tile([P, BANK], F32, name="product", tag="product", bufs=4)
+
+        def multiply(dst, w_codes, w_scales, cell_codes, cell_scales):
+            nc.tensor.matmul_mx(
+                out=dst,
+                lhsT=w_codes.bitcast(FP8X4),
+                lhsT_scale=w_scales,
+                rhs=cell_codes.bitcast(FP8X4),
+                rhs_scale=cell_scales,
+                start=True,
+                stop=True,
+            )
+
+        offs_t = keep.tile([P, S // GROUP], U16, name="offs_t")
+        p1_t = keep.tile([P, S // GROUP], U16, name="p1_t")
+        p2_t = keep.tile([P, S // GROUP], U16, name="p2_t")
         w1_raw = keep.tile([P, PACK, H], F32, name="w1_raw")
         w2_raw = keep.tile([P, PACK, N], F32, name="w2_raw")
-        xw = keep.tile([P, T], I32, name="xw")
-        xs = keep.tile([P, T], U8, name="xs")
+        all_words = keep.tile([P, T], I32, name="all_words")
+        all_scales = keep.tile([P, T], U8, name="all_scales")
         gain = keep.tile([P, PACK], F32, name="gain")
 
-        nc.vector.memset(xs[:].bitcast(I32), 0)
-        warm_in = keep.tile([P, 1], F32, name="warm_in")
-        warm_out = keep.tile([P, 1], F32, name="warm_out")
-        nc.vector.memset(warm_in[:], 0.0)
-        nc.scalar.activation(warm_out[:], warm_in[:], ACT.Exp)
-
+        nc.vector.memset(all_scales[:].bitcast(I32), 0)
         nc.sync.dma_start(offs_t[:], offs)
         nc.sync.dma_start(w1_raw[:], w1.rearrange("(p j) h -> p j h", j=PACK))
         for q in range(4):
-            nc.sync.dma_start(xs[32 * q : 32 * q + 4, :].bitcast(I32), x_scales[0, 4 * q : 4 * q + 4, :].bitcast(I32))
-        nc.sync.dma_start(xw[:], x_words[0].rearrange("p n t -> p (n t)").bitcast(I32))
+            nc.sync.dma_start(
+                all_scales[32 * q : 32 * q + 4, :].bitcast(I32), x_scales[0, 4 * q : 4 * q + 4, :].bitcast(I32)
+            )
+        nc.sync.dma_start(all_words[:], x_words[0].rearrange("p n t -> p (n t)").bitcast(I32))
         nc.scalar.dma_start(gain[:], gn.rearrange("(p t) o -> p (t o)", t=PACK))
         nc.sync.dma_start(p1_t[:], p1)
         nc.sync.dma_start(p2_t[:], p2)
@@ -56,8 +70,8 @@ def tile_picked_perona_none_p_kernel(tc, x_words, x_scales, w1, gn, w2, offs, p1
         ident = keep.tile([P, P], F32, name="ident")
         make_identity(nc, ident[:])
 
-        xg_scales = keep.tile([P, S], U8, name="xg_scales", align_bytes=64)
-        nc.vector.tensor_copy(xg_scales[:], xs[:].indirect(offs_t[:]))
+        picked_scales = keep.tile([P, S], U8, name="picked_scales", align_bytes=64)
+        nc.vector.tensor_copy(picked_scales[:], all_scales[:].indirect(offs_t[:]))
 
         gain_safe = keep.tile([P, PACK], F32, name="gain_safe")
         inv_gain = keep.tile([P, PACK], F32, name="inv_gain")
@@ -65,220 +79,185 @@ def tile_picked_perona_none_p_kernel(tc, x_words, x_scales, w1, gn, w2, offs, p1
         nc.vector.reciprocal(inv_gain[:], gain_safe[:])
 
         w1_codes, w1_scales = [], []
-        w1_view = w1_raw[:].rearrange("p j (m t) -> p m t j", t=PACK)
-        for h in range(2):
-            grouped = keep.tile([P, 2, P, PACK], BF16, name=f"w1_grouped{h}", align_bytes=64)
-            dst = grouped[:].rearrange("p t m j -> p m t j")
-            src = w1_view[:, :, 2 * h : 2 * h + 2, :]
-            if h == 0:
-                nc.vector.tensor_copy(dst, src)
-            else:
-                nc.scalar.copy(dst, src)
-            codes = keep.tile([P, 2 * P], U32, name=f"w1_codes{h}", align_bytes=64)
-            scales = keep.tile([P, 2 * P], U8, name=f"w1_scales{h}", align_bytes=64)
-            nc.vector.quantize_mx(out=codes[:].bitcast(FP8X4), scales=scales[:], in_=grouped[:].rearrange("p t m j -> p (t m j)"))
+        w1_dealt = w1_raw[:].rearrange("p j (m t) -> p m t j", t=PACK)
+        for pair, copy in enumerate((nc.vector.tensor_copy, nc.scalar.copy)):
+            grouped = keep.tile([P, 2, P, PACK], BF16, name=f"w1_grouped{pair}", align_bytes=64)
+            copy(grouped[:].rearrange("p t m j -> p m t j"), w1_dealt[:, :, 2 * pair : 2 * pair + 2, :])
+            codes = keep.tile([P, 2 * P], U32, name=f"w1_codes{pair}", align_bytes=64)
+            scales = keep.tile([P, 2 * P], U8, name=f"w1_scales{pair}", align_bytes=64)
+            nc.vector.quantize_mx(
+                out=codes[:].bitcast(FP8X4), scales=scales[:], in_=grouped[:].rearrange("p t m j -> p (t m j)")
+            )
             w1_codes.append(codes)
             w1_scales.append(scales)
 
-        xg_words = keep.tile([P, S], U32, name="xg_words", align_bytes=64)
+        picked_words = keep.tile([P, S], U32, name="picked_words", align_bytes=64)
         half = S // 2
-        for a in range(2):
+        for c0 in (0, half):
             nc.vector.tensor_copy(
-                xg_words[:, a * half : (a + 1) * half],
-                xw[:].bitcast(U32).indirect(offs_t[:, a * half // 16 : (a + 1) * half // 16]),
+                picked_words[:, c0 : c0 + half],
+                all_words[:].bitcast(U32).indirect(offs_t[:, c0 // GROUP : (c0 + half) // GROUP]),
             )
 
-        yg = [keep.tile([P, S], F32, name=f"yg{t}") for t in range(PACK)]
-        first = CHUNKS[0][1]
-        y_head = [keep.tile([P, first], F32, name=f"y_head{t}") for t in range(PACK)]
-        y_rest = keep.tile([P, PACK, S - first], F32, name="y_rest")
+        planes = [keep.tile([P, S], F32, name=f"plane{t}") for t in range(PACK)]
+        n_first = CHUNKS[0][1]
+        own_first = [keep.tile([P, n_first], F32, name=f"own_first{t}") for t in range(PACK)]
+        own_later = keep.tile([P, PACK, S - n_first], F32, name="own_later")
 
         def first_product(t, c0, c1):
-            bank = psum.tile([P, 512], F32, name="bank", tag="mx", bufs=4)
+            bank = product_bank()
             cols = slice((t % 2) * P, (t % 2 + 1) * P)
-            nc.tensor.matmul_mx(
-                out=bank[:, 0 : c1 - c0],
-                lhsT=w1_codes[t // 2][:, cols].bitcast(FP8X4),
-                lhsT_scale=w1_scales[t // 2][:, cols],
-                rhs=xg_words[:, c0:c1].bitcast(FP8X4),
-                rhs_scale=xg_scales[:, c0:c1],
-                start=True,
-                stop=True,
+            multiply(
+                bank[:, 0 : c1 - c0],
+                w1_codes[t // 2][:, cols],
+                w1_scales[t // 2][:, cols],
+                picked_words[:, c0:c1],
+                picked_scales[:, c0:c1],
             )
-            nc.scalar.activation(yg[t][:, c0:c1], bank[:, 0 : c1 - c0], ACT.Copy, scale=gain[:, t : t + 1])
+            nc.scalar.activation(planes[t][:, c0:c1], bank[:, 0 : c1 - c0], ACT.Copy, scale=gain[:, t : t + 1])
 
         first_product(0, 0, half)
-        nc.vector.tensor_copy(y_head[0][:], yg[0][:, 0:first])
+        nc.vector.tensor_copy(own_first[0][:], planes[0][:, 0:n_first])
         first_product(0, half, S)
-        nc.sync.dma_start(y_rest[:, 0, :], yg[0][:, first:S])
+        nc.sync.dma_start(own_later[:, 0, :], planes[0][:, n_first:S])
         for t in range(1, PACK):
             first_product(t, 0, S)
-            nc.sync.dma_start(y_rest[:, t, :], yg[t][:, first:S])
+            nc.sync.dma_start(own_later[:, t, :], planes[t][:, n_first:S])
 
         w2_codes = keep.tile([P, N], U32, name="w2_codes", align_bytes=64)
         w2_scales = keep.tile([P, N], U8, name="w2_scales", align_bytes=64)
 
-        def quantize_w2(a):
-            cols = slice(a * 256, (a + 1) * 256)
-            grouped = keep.tile([P, 256 * PACK], BF16, name=f"w2_grouped{a}", align_bytes=64)
-            dst = grouped[:].rearrange("p (c i t) -> p c t i", i=4, t=PACK)
-            src = w2_raw[:, :, cols].rearrange("p t (c i) -> p c t i", i=4)
-            if a < 2:
-                nc.scalar.copy(dst, src)
-            else:
-                nc.vector.tensor_copy(dst, src)
+        def quantize_w2(part):
+            cols = slice(part * N // 2, (part + 1) * N // 2)
+            grouped = keep.tile([P, N // 2 * PACK], BF16, name=f"w2_grouped{part}", align_bytes=64)
+            nc.scalar.copy(
+                grouped[:].rearrange("p (c i j) -> p c j i", i=LINE, j=PACK),
+                w2_raw[:, :, cols].rearrange("p j (c i) -> p c j i", i=LINE),
+            )
             nc.vector.quantize_mx(out=w2_codes[:, cols].bitcast(FP8X4), scales=w2_scales[:, cols], in_=grouped[:])
 
         last = len(CHUNKS) - 1
-        units = [(c, (t,)) for c in range(3) for t in range(4)]
-        slots = [keep.tile([P, 512], F32, name=f"slot{i}") for i in range(len(units) + LEAD)]
-        sums, packed = {}, {}
-
-        def plain_y(c, t):
-            j0, n = CHUNKS[c]
-            return y_head[t][:] if c == 0 else y_rest[:, t, j0 - first : j0 - first + n]
+        n_last = CHUNKS[last][1]
+        units = [(c, t) for c in range(len(CHUNKS)) for t in range(PACK)]
+        widths = [2 * CHUNKS[c][1] for c, t in units]
+        slots = [keep.tile([P, max(widths)], F32, name=f"slot{i}") for i in range(len(units) + LEAD)]
+        last_terms = keep.tile([P, PACK * 2 * n_last], F32, name="last_terms")
+        last_by_list = last_terms[:].rearrange("p (t s j) -> p t s j", t=PACK, s=2)
+        last_partial = keep.tile([P, PACK, n_last], F32, name="last_partial")
+        weights = [keep.tile([P, w], F32, name=f"weight{i}") for i, w in enumerate(widths)]
+        terms = [
+            last_terms[:, widths[i] * t : widths[i] * (t + 1)] if c == last else keep.tile([P, widths[i]], F32, name=f"term{i}")
+            for i, (c, t) in enumerate(units)
+        ]
+        sums = {}
 
         def gather(i):
-            c, planes = units[i]
+            c, t = units[i]
             j0, n = CHUNKS[c]
-            for k, t in enumerate(planes):
-                for s, lists in enumerate((p1_t, p2_t)):
-                    nc.vector.tensor_tensor(
-                        slots[i][:, (2 * k + s) * n : (2 * k + s + 1) * n],
-                        yg[t][:].indirect(lists[:, j0 // 16 : (j0 + n) // 16]),
-                        plain_y(c, t),
-                        ALU.subtract,
-                    )
+            own = own_first[t][:] if c == 0 else own_later[:, t, j0 - n_first : j0 - n_first + n]
+            for s, lists in enumerate((p1_t, p2_t)):
+                nc.vector.tensor_tensor(
+                    slots[i][:, s * n : (s + 1) * n],
+                    planes[t][:].indirect(lists[:, j0 // GROUP : (j0 + n) // GROUP]),
+                    own,
+                    ALU.subtract,
+                )
 
         def weigh(i, cols):
-            c, planes = units[i]
-            step = (cols.stop - cols.start) // len(planes)
-            for k, t in enumerate(planes):
-                part = slice(cols.start + k * step, cols.start + (k + 1) * step)
-                nc.scalar.activation(slots[i + LEAD][:, part], slots[i][:, part], ACT.Square, scale=inv_gain[:, t : t + 1])
+            t = units[i][1]
+            nc.scalar.activation(slots[i + LEAD][:, cols], slots[i][:, cols], ACT.Square, scale=inv_gain[:, t : t + 1])
             nc.scalar.activation(weights[i][:, cols], slots[i + LEAD][:, cols], ACT.Exp, scale=-0.5)
 
         def pull(i, cols):
-            nc.vector.scalar_tensor_tensor(pulls[i][:, cols], weights[i][:, cols], 0.25, slots[i][:, cols], ALU.mult, ALU.mult)
+            nc.vector.scalar_tensor_tensor(terms[i][:, cols], weights[i][:, cols], 0.25, slots[i][:, cols], ALU.mult, ALU.mult)
 
         def add_turned(i):
-            c, planes = units[i]
+            c, t = units[i]
             j0, n = CHUNKS[c]
-            for k, t in enumerate(planes):
-                for b in range(n // P):
-                    if t == 0:
-                        sums[c, b] = psum.tile([P, PACK, P], F32, name="zt", tag="zt", bufs=3)
-                    terms = (
-                        yg[t][:, j0 + b * P : j0 + (b + 1) * P],
-                        pulls[i][:, 2 * k * n + b * P : 2 * k * n + (b + 1) * P],
-                        pulls[i][:, (2 * k + 1) * n + b * P : (2 * k + 1) * n + (b + 1) * P],
+            for b in range(n // P):
+                if t == 0:
+                    sums[c, b] = psum.tile([P, PACK, P], F32, name="sum", tag="sum", bufs=3)
+                parts = (
+                    planes[t][:, j0 + b * P : j0 + (b + 1) * P],
+                    terms[i][:, b * P : (b + 1) * P],
+                    terms[i][:, n + b * P : n + (b + 1) * P],
+                )
+                for a, part in enumerate(parts):
+                    nc.tensor.matmul(
+                        sums[c, b][:, t, :], part, ident[:], start=(a == 0), stop=(a == len(parts) - 1), is_transpose=True
                     )
-                    for a, term in enumerate(terms):
-                        nc.tensor.matmul(sums[c, b][:, t, :], term, ident[:], start=(a == 0), stop=(a == 2), is_transpose=True)
-
-        n_last = CHUNKS[last][1]
-        m_last = keep.tile([P, PACK * 2 * n_last], F32, name="m_last")
-        m_view = m_last[:].rearrange("p (t s j) -> p t s j", t=PACK, s=2)
-        a_last = keep.tile([P, PACK, n_last], F32, name="a_last")
-        widths = [2 * len(planes) * CHUNKS[c][1] for c, planes in units]
-        weights = [keep.tile([P, w], F32, name=f"e{i}") for i, w in enumerate(widths)]
-        pulls = [
-            m_last[:, 2 * n_last * planes[0] : 2 * n_last * (planes[-1] + 1)] if c == last else keep.tile([P, widths[i]], F32, name=f"m{i}")
-            for i, (c, planes) in enumerate(units)
-        ]
-
-        def add_first(ts):
-            nc.vector.tensor_tensor(a_last[:, ts, :], m_view[:, ts, 0, :], y_rest[:, ts, S - first - n_last : S - first], ALU.add)
-
-        def quantize_z(c, z):
-            n = CHUNKS[c][1]
-            z_codes = keep.tile([P, n], U32, name=f"z_codes{c}", align_bytes=64)
-            z_scales = keep.tile([P, n], U8, name=f"z_scales{c}", align_bytes=64)
-            nc.vector.quantize_mx(out=z_codes[:].bitcast(FP8X4), scales=z_scales[:], in_=z[:])
-            packed[c] = (z_codes, z_scales)
 
         def turn_back(c):
             n = CHUNKS[c][1]
             blocks = n // P
-            back = psum.tile([P, 2, 2, P], F32, name="back", tag="back", bufs=1)
+            back = psum.tile([P, n_first // P, 2, P], F32, name="back", tag="back", bufs=1)
             for b in range(blocks):
-                zt = keep.tile([P, 2, P, 2], BF16, name=f"zt{c}_{b}")
-                nc.scalar.copy(zt[:], sums[c, b][:].rearrange("j (u e) p -> j u p e", e=2))
-                words = zt[:].rearrange("j u p e -> j (u p e)").bitcast(F32)
+                rounded = keep.tile([P, 2, P, 2], BF16, name=f"rounded{c}_{b}")
+                nc.scalar.copy(rounded[:], sums[c, b][:].rearrange("j (u e) p -> j u p e", e=2))
+                pairs = rounded[:].rearrange("j u p e -> j (u p e)").bitcast(F32)
                 for u in range(2):
-                    nc.tensor.transpose(back[:, b, u, :], words[:, u * P : (u + 1) * P], ident[:])
+                    nc.tensor.transpose(back[:, b, u, :], pairs[:, u * P : (u + 1) * P], ident[:])
             z = keep.tile([P, n * PACK], BF16, name=f"z{c}", align_bytes=64)
-            z_dst = z[:].bitcast(F32).rearrange("p (b j u) -> p b j u", b=blocks, u=2)
-            z_src = back[:, 0:blocks, :, :].rearrange("p b u j -> p b j u")
-            if c in ():
-                nc.vector.tensor_copy(z_dst, z_src)
-            else:
-                nc.scalar.copy(z_dst, z_src)
-            quantize_z(c, z)
+            nc.scalar.copy(
+                z[:].bitcast(F32).rearrange("p (b j u) -> p b j u", b=blocks, u=2),
+                back[:, 0:blocks, :, :].rearrange("p b u j -> p b j u"),
+            )
+            return z
 
-        def second_product(c, on_vector):
+        def second_product(c, z, ways):
             j0, n = CHUNKS[c]
-            z_codes, z_scales = packed[c]
-            per_bank = 2 if c == last else 512 // n
-            for g in range(PACK // per_bank):
-                bank = psum.tile([P, 512], F32, name="bank", tag="mx", bufs=4)
-                for i in range(per_bank):
-                    rows = slice((g * per_bank + i) * P, (g * per_bank + i + 1) * P)
-                    nc.tensor.matmul_mx(
-                        out=bank[:, i * n : (i + 1) * n],
-                        lhsT=w2_codes[:, rows].bitcast(FP8X4),
-                        lhsT_scale=w2_scales[:, rows],
-                        rhs=z_codes[:].bitcast(FP8X4),
-                        rhs_scale=z_scales[:],
-                        start=True,
-                        stop=True,
-                    )
-                res = keep.tile([P, per_bank, n], F32, name=f"res{c}_{g}")
-                res_dst = res[:].rearrange("p a j -> p (a j)")
+            z_codes = keep.tile([P, n], U32, name=f"z_codes{c}", align_bytes=64)
+            z_scales = keep.tile([P, n], U8, name=f"z_scales{c}", align_bytes=64)
+            nc.vector.quantize_mx(out=z_codes[:].bitcast(FP8X4), scales=z_scales[:], in_=z[:])
+            per_bank = N // P // len(ways)
+            for g, (copy, store) in enumerate(ways):
+                bank = product_bank()
+                for a in range(per_bank):
+                    rows = slice((g * per_bank + a) * P, (g * per_bank + a + 1) * P)
+                    multiply(bank[:, a * n : (a + 1) * n], w2_codes[:, rows], w2_scales[:, rows], z_codes[:], z_scales[:])
+                result = keep.tile([P, per_bank, n], F32, name=f"result{c}_{g}")
+                copy(result[:].rearrange("p a j -> p (a j)"), bank[:, 0 : per_bank * n])
                 r0 = g * per_bank * P
-                rows_out = out[r0 : r0 + per_bank * P, j0 : j0 + n].rearrange("(a p) j -> p a j", p=P)
-                if g in on_vector:
-                    nc.vector.tensor_copy(res_dst, bank[:, 0 : per_bank * n])
-                else:
-                    nc.scalar.copy(res_dst, bank[:, 0 : per_bank * n])
-                if c == last and g not in on_vector:
-                    nc.scalar.dma_start(rows_out, res[:])
-                else:
-                    nc.sync.dma_start(rows_out, res[:])
+                store(out[r0 : r0 + per_bank * P, j0 : j0 + n].rearrange("(a p) j -> p a j", p=P), result[:])
+
+        ways_out = (
+            [(nc.vector.tensor_copy, nc.sync.dma_start)] * 2,
+            [(nc.scalar.copy, nc.sync.dma_start)],
+            [(nc.vector.tensor_copy, nc.sync.dma_start), (nc.scalar.copy, nc.scalar.dma_start)],
+        )
 
         final = len(units) - 1
         for i in range(len(units) + 1):
             if i + 1 < PACK:
-                nc.vector.tensor_copy(y_head[i + 1][:], yg[i + 1][:, 0:first])
+                nc.vector.tensor_copy(own_first[i + 1][:], planes[i + 1][:, 0:n_first])
             if i <= final:
                 gather(i)
             if 1 <= i <= final:
                 weigh(i - 1, slice(0, widths[i - 1]))
-            if i == 1:
-                quantize_w2(0)
-            if i == 2:
-                quantize_w2(1)
+            if i in (1, 2):
+                quantize_w2(i - 1)
             if i >= 2:
                 pull(i - 2, slice(0, widths[i - 2]))
-                if units[i - 2][0] < last:
+                c, t = units[i - 2]
+                if c < last:
                     add_turned(i - 2)
-            if i >= 3 and units[i - 3][1][-1] == PACK - 1 and units[i - 3][0] < last:
-                turn_back(units[i - 3][0])
-            if i >= 4 and units[i - 4][1][-1] == PACK - 1 and units[i - 4][0] < last - 1:
-                second_product(units[i - 4][0], (0, 1))
-        weigh(final, slice(0, n_last))
-        weigh(final, slice(n_last, 2 * n_last))
-        pull(final, slice(0, n_last))
-        pull(final, slice(n_last, 2 * n_last))
-        add_first(slice(0, PACK - 1))
-        add_first(slice(PACK - 1, PACK))
-        z = keep.tile([P, n_last * PACK], BF16, name="z_last", align_bytes=64)
+                if c < last and t == PACK - 1:
+                    second_product(c, turn_back(c), ways_out[c])
+
+        halves = (slice(0, n_last), slice(n_last, 2 * n_last))
+        for cols in halves:
+            weigh(final, cols)
+        for cols in halves:
+            pull(final, cols)
+        for ts in (slice(0, PACK - 1), slice(PACK - 1, PACK)):
+            nc.vector.tensor_tensor(
+                last_partial[:, ts, :], last_by_list[:, ts, 0, :], own_later[:, ts, S - n_first - n_last : S - n_first], ALU.add
+            )
+        z_last = keep.tile([P, n_last * PACK], BF16, name="z_last", align_bytes=64)
         nc.vector.tensor_tensor(
-            z[:].rearrange("p (c i t) -> p c t i", i=4, t=PACK),
-            m_view[:, :, 1, :].rearrange("p t (c i) -> p c t i", i=4),
-            a_last[:].rearrange("p t (c i) -> p c t i", i=4),
+            z_last[:].rearrange("p (c i t) -> p c t i", i=LINE, t=PACK),
+            last_by_list[:, :, 1, :].rearrange("p t (c i) -> p c t i", i=LINE),
+            last_partial[:].rearrange("p t (c i) -> p c t i", i=LINE),
             ALU.add,
         )
-        quantize_z(last, z)
-        second_product(last - 1, ())
-        second_product(last, (0,))
+        second_product(last, z_last, ways_out[last])

from contextlib import ExitStack

import concourse.mybir as mybir
from concourse.masks import make_identity

K, T, S, N, H = 512, 2048, 512, 512, 512
FLOPS = 2 * K * H * S + 2 * H * N * S

F32 = mybir.dt.float32
BF16 = mybir.dt.bfloat16
I32 = mybir.dt.int32
U32 = mybir.dt.uint32
U16 = mybir.dt.uint16
U8 = mybir.dt.uint8
FP8X4 = mybir.dt.float8_e4m3fn_x4
ALU = mybir.AluOpType
ACT = mybir.ActivationFunctionType

P = 128
PACK = 4
BANK = 512
GROUP = 16
LINE = 4
CHUNKS = ((0, 256), (256, 128), (384, 128))
LEAD = 4


def tile_picked_perona_none_p_kernel(tc, x_words, x_scales, w1, gn, w2, offs, p1, p2, out):
    nc = tc.nc
    with ExitStack() as ctx:
        keep = ctx.enter_context(tc.tile_pool(name="keep", bufs=1))
        psum = ctx.enter_context(tc.psum_pool(name="psum", bufs=1))

        def product_bank():
            return psum.tile([P, BANK], F32, name="product", tag="product", bufs=4)

        def multiply(dst, w_codes, w_scales, cell_codes, cell_scales):
            nc.tensor.matmul_mx(
                out=dst,
                lhsT=w_codes.bitcast(FP8X4),
                lhsT_scale=w_scales,
                rhs=cell_codes.bitcast(FP8X4),
                rhs_scale=cell_scales,
                start=True,
                stop=True,
            )

        offs_t = keep.tile([P, S // GROUP], U16, name="offs_t")
        p1_t = keep.tile([P, S // GROUP], U16, name="p1_t")
        p2_t = keep.tile([P, S // GROUP], U16, name="p2_t")
        w1_raw = keep.tile([P, PACK, H], F32, name="w1_raw")
        w2_raw = keep.tile([P, PACK, N], F32, name="w2_raw")
        all_words = keep.tile([P, T], I32, name="all_words")
        all_scales = keep.tile([P, T], U8, name="all_scales")
        gain = keep.tile([P, PACK], F32, name="gain")

        nc.vector.memset(all_scales[:].bitcast(I32), 0)
        nc.sync.dma_start(offs_t[:], offs)
        nc.sync.dma_start(w1_raw[:], w1.rearrange("(p j) h -> p j h", j=PACK))
        for q in range(4):
            nc.sync.dma_start(
                all_scales[32 * q : 32 * q + 4, :].bitcast(I32), x_scales[0, 4 * q : 4 * q + 4, :].bitcast(I32)
            )
        nc.sync.dma_start(all_words[:], x_words[0].rearrange("p n t -> p (n t)").bitcast(I32))
        nc.scalar.dma_start(gain[:], gn.rearrange("(p t) o -> p (t o)", t=PACK))
        nc.sync.dma_start(p1_t[:], p1)
        nc.sync.dma_start(p2_t[:], p2)
        nc.sync.dma_start(w2_raw[:], w2.rearrange("(p j) n -> p j n", j=PACK))

        ident = keep.tile([P, P], F32, name="ident")
        make_identity(nc, ident[:])

        picked_scales = keep.tile([P, S], U8, name="picked_scales", align_bytes=64)
        nc.vector.tensor_copy(picked_scales[:], all_scales[:].indirect(offs_t[:]))

        gain_safe = keep.tile([P, PACK], F32, name="gain_safe")
        inv_gain = keep.tile([P, PACK], F32, name="inv_gain")
        nc.vector.scalar_tensor_tensor(gain_safe[:], gain[:], 0.0, gain[:], ALU.is_equal, ALU.add)
        nc.vector.reciprocal(inv_gain[:], gain_safe[:])

        w1_codes, w1_scales = [], []
        w1_dealt = w1_raw[:].rearrange("p j (m t) -> p m t j", t=PACK)
        for pair, copy in enumerate((nc.vector.tensor_copy, nc.scalar.copy)):
            grouped = keep.tile([P, 2, P, PACK], BF16, name=f"w1_grouped{pair}", align_bytes=64)
            copy(grouped[:].rearrange("p t m j -> p m t j"), w1_dealt[:, :, 2 * pair : 2 * pair + 2, :])
            codes = keep.tile([P, 2 * P], U32, name=f"w1_codes{pair}", align_bytes=64)
            scales = keep.tile([P, 2 * P], U8, name=f"w1_scales{pair}", align_bytes=64)
            nc.vector.quantize_mx(
                out=codes[:].bitcast(FP8X4), scales=scales[:], in_=grouped[:].rearrange("p t m j -> p (t m j)")
            )
            w1_codes.append(codes)
            w1_scales.append(scales)

        picked_words = keep.tile([P, S], U32, name="picked_words", align_bytes=64)
        half = S // 2
        for c0 in (0, half):
            nc.vector.tensor_copy(
                picked_words[:, c0 : c0 + half],
                all_words[:].bitcast(U32).indirect(offs_t[:, c0 // GROUP : (c0 + half) // GROUP]),
            )

        planes = [keep.tile([P, S], F32, name=f"plane{t}") for t in range(PACK)]
        n_first = CHUNKS[0][1]
        own_first = [keep.tile([P, n_first], F32, name=f"own_first{t}") for t in range(PACK)]
        own_later = keep.tile([P, PACK, S - n_first], F32, name="own_later")

        def first_product(t, c0, c1):
            bank = product_bank()
            cols = slice((t % 2) * P, (t % 2 + 1) * P)
            multiply(
                bank[:, 0 : c1 - c0],
                w1_codes[t // 2][:, cols],
                w1_scales[t // 2][:, cols],
                picked_words[:, c0:c1],
                picked_scales[:, c0:c1],
            )
            nc.scalar.activation(planes[t][:, c0:c1], bank[:, 0 : c1 - c0], ACT.Copy, scale=gain[:, t : t + 1])

        first_product(0, 0, half)
        nc.vector.tensor_copy(own_first[0][:], planes[0][:, 0:n_first])
        first_product(0, half, S)
        nc.sync.dma_start(own_later[:, 0, :], planes[0][:, n_first:S])
        for t in range(1, PACK):
            first_product(t, 0, S)
            nc.sync.dma_start(own_later[:, t, :], planes[t][:, n_first:S])

        w2_codes = keep.tile([P, N], U32, name="w2_codes", align_bytes=64)
        w2_scales = keep.tile([P, N], U8, name="w2_scales", align_bytes=64)

        def quantize_w2(part):
            cols = slice(part * N // 2, (part + 1) * N // 2)
            grouped = keep.tile([P, N // 2 * PACK], BF16, name=f"w2_grouped{part}", align_bytes=64)
            nc.scalar.copy(
                grouped[:].rearrange("p (c i j) -> p c j i", i=LINE, j=PACK),
                w2_raw[:, :, cols].rearrange("p j (c i) -> p c j i", i=LINE),
            )
            nc.vector.quantize_mx(out=w2_codes[:, cols].bitcast(FP8X4), scales=w2_scales[:, cols], in_=grouped[:])

        last = len(CHUNKS) - 1
        n_last = CHUNKS[last][1]
        units = [(c, t) for c in range(len(CHUNKS)) for t in range(PACK)]
        widths = [2 * CHUNKS[c][1] for c, t in units]
        slots = [keep.tile([P, max(widths)], F32, name=f"slot{i}") for i in range(len(units) + LEAD)]
        last_terms = keep.tile([P, PACK * 2 * n_last], F32, name="last_terms")
        last_by_list = last_terms[:].rearrange("p (t s j) -> p t s j", t=PACK, s=2)
        last_partial = keep.tile([P, PACK, n_last], F32, name="last_partial")
        weights = [keep.tile([P, w], F32, name=f"weight{i}") for i, w in enumerate(widths)]
        terms = [
            last_terms[:, widths[i] * t : widths[i] * (t + 1)] if c == last else keep.tile([P, widths[i]], F32, name=f"term{i}")
            for i, (c, t) in enumerate(units)
        ]
        sums = {}

        def gather(i):
            c, t = units[i]
            j0, n = CHUNKS[c]
            own = own_first[t][:] if c == 0 else own_later[:, t, j0 - n_first : j0 - n_first + n]
            for s, lists in enumerate((p1_t, p2_t)):
                nc.vector.tensor_tensor(
                    slots[i][:, s * n : (s + 1) * n],
                    planes[t][:].indirect(lists[:, j0 // GROUP : (j0 + n) // GROUP]),
                    own,
                    ALU.subtract,
                )

        def weigh(i, cols):
            t = units[i][1]
            nc.scalar.activation(slots[i + LEAD][:, cols], slots[i][:, cols], ACT.Square, scale=inv_gain[:, t : t + 1])
            nc.scalar.activation(weights[i][:, cols], slots[i + LEAD][:, cols], ACT.Exp, scale=-0.5)

        def pull(i, cols):
            nc.vector.scalar_tensor_tensor(terms[i][:, cols], weights[i][:, cols], 0.25, slots[i][:, cols], ALU.mult, ALU.mult)

        def add_turned(i):
            c, t = units[i]
            j0, n = CHUNKS[c]
            for b in range(n // P):
                if t == 0:
                    sums[c, b] = psum.tile([P, PACK, P], F32, name="sum", tag="sum", bufs=3)
                parts = (
                    planes[t][:, j0 + b * P : j0 + (b + 1) * P],
                    terms[i][:, b * P : (b + 1) * P],
                    terms[i][:, n + b * P : n + (b + 1) * P],
                )
                for a, part in enumerate(parts):
                    nc.tensor.matmul(
                        sums[c, b][:, t, :], part, ident[:], start=(a == 0), stop=(a == len(parts) - 1), is_transpose=True
                    )

        def turn_back(c):
            n = CHUNKS[c][1]
            blocks = n // P
            back = psum.tile([P, n_first // P, 2, P], F32, name="back", tag="back", bufs=1)
            for b in range(blocks):
                rounded = keep.tile([P, 2, P, 2], BF16, name=f"rounded{c}_{b}")
                nc.scalar.copy(rounded[:], sums[c, b][:].rearrange("j (u e) p -> j u p e", e=2))
                pairs = rounded[:].rearrange("j u p e -> j (u p e)").bitcast(F32)
                for u in range(2):
                    nc.tensor.transpose(back[:, b, u, :], pairs[:, u * P : (u + 1) * P], ident[:])
            z = keep.tile([P, n * PACK], BF16, name=f"z{c}", align_bytes=64)
            nc.scalar.copy(
                z[:].bitcast(F32).rearrange("p (b j u) -> p b j u", b=blocks, u=2),
                back[:, 0:blocks, :, :].rearrange("p b u j -> p b j u"),
            )
            return z

        def second_product(c, z, ways):
            j0, n = CHUNKS[c]
            z_codes = keep.tile([P, n], U32, name=f"z_codes{c}", align_bytes=64)
            z_scales = keep.tile([P, n], U8, name=f"z_scales{c}", align_bytes=64)
            nc.vector.quantize_mx(out=z_codes[:].bitcast(FP8X4), scales=z_scales[:], in_=z[:])
            per_bank = N // P // len(ways)
            for g, (copy, store) in enumerate(ways):
                bank = product_bank()
                for a in range(per_bank):
                    rows = slice((g * per_bank + a) * P, (g * per_bank + a + 1) * P)
                    multiply(bank[:, a * n : (a + 1) * n], w2_codes[:, rows], w2_scales[:, rows], z_codes[:], z_scales[:])
                result = keep.tile([P, per_bank, n], F32, name=f"result{c}_{g}")
                copy(result[:].rearrange("p a j -> p (a j)"), bank[:, 0 : per_bank * n])
                r0 = g * per_bank * P
                store(out[r0 : r0 + per_bank * P, j0 : j0 + n].rearrange("(a p) j -> p a j", p=P), result[:])

        ways_out = (
            [(nc.vector.tensor_copy, nc.sync.dma_start)] * 2,
            [(nc.scalar.copy, nc.sync.dma_start)],
            [(nc.vector.tensor_copy, nc.sync.dma_start), (nc.scalar.copy, nc.scalar.dma_start)],
        )

        final = len(units) - 1
        for i in range(len(units) + 1):
            if i + 1 < PACK:
                nc.vector.tensor_copy(own_first[i + 1][:], planes[i + 1][:, 0:n_first])
            if i <= final:
                gather(i)
            if 1 <= i <= final:
                weigh(i - 1, slice(0, widths[i - 1]))
            if i in (1, 2):
                quantize_w2(i - 1)
            if i >= 2:
                pull(i - 2, slice(0, widths[i - 2]))
                c, t = units[i - 2]
                if c < last:
                    add_turned(i - 2)
                if c < last and t == PACK - 1:
                    second_product(c, turn_back(c), ways_out[c])

        halves = (slice(0, n_last), slice(n_last, 2 * n_last))
        for cols in halves:
            weigh(final, cols)
        for cols in halves:
            pull(final, cols)
        for ts in (slice(0, PACK - 1), slice(PACK - 1, PACK)):
            nc.vector.tensor_tensor(
                last_partial[:, ts, :], last_by_list[:, ts, 0, :], own_later[:, ts, S - n_first - n_last : S - n_first], ALU.add
            )
        z_last = keep.tile([P, n_last * PACK], BF16, name="z_last", align_bytes=64)
        nc.vector.tensor_tensor(
            z_last[:].rearrange("p (c i t) -> p c t i", i=LINE, t=PACK),
            last_by_list[:, :, 1, :].rearrange("p t (c i) -> p c t i", i=LINE),
            last_partial[:].rearrange("p t (c i) -> p c t i", i=LINE),
            ALU.add,
        )
        second_product(last, z_last, ways_out[last])
